import numpy as np, ml_dtypes
CORES = [33,38,57,62,81,86,161,166,185,190,209,214]
N = 12
import mx_ref
NC, KT, ROOT = 256, 2, 5
BF = ml_dtypes.bfloat16
def cut(t, i, w=512):
    return t[:, w * i:w * i + w]
def pk(c, s, i=0):
    return (np.ascontiguousarray(c[:, 512 * i:512 * i + 512]), mx_ref.live(s[:, 128 * i:128 * i + 128]))
def inputs(rng, e, E):
    def f(*shape):
        v = (rng.standard_normal(shape, dtype=np.float32) * np.exp2(rng.integers(-2, 3, shape[:-1] + (1,)))).astype(BF)
        return mx_ref.spread((v.astype(np.float32) * np.exp2(rng.integers(-E, E + 1, shape[:-2] + (1, 1))).astype(np.float32)).astype(BF), rng, e)
    def packed(k):
        c = np.zeros((N, 128, k * 512), np.uint8); s = np.zeros((N, 128, k * 128), np.uint8)
        for r in range(N):
            for i in range(k):
                a, b = mx_ref.quantize(f(128, 512)); c[r][:, 512 * i:512 * i + 512] = a; s[r][:, 128 * i:128 * i + 128] = mx_ref.plane(b, rng)
        return c, s
    d = {}
    d["wc"], d["ws"] = packed(KT)
    d["x"] = f(N, 128, KT * 4 * NC)
    return d
def setup_inputs(rng):
    return inputs(rng, 0, 0)
def setup_inputs_blocks(rng):
    return inputs(rng, 4, 0)
def setup_inputs_wide(rng):
    return inputs(rng, 0, 8)
def reference(wc, ws, x):
    y = np.zeros((N, 128, NC), np.float32)
    for r in range(N):
        for t in range(KT):
            p = mx_ref.matmul(pk(wc[ROOT], ws[ROOT], t), mx_ref.quantize(cut(x[r], t, 4 * NC)))
            y[r] = p if t == 0 else y[r] + p
    return {"y": y}

@@ -1,0 +1,212 @@
+from concourse.bass import DstId, RemoteDMATransfer
+from concourse.mybir import dt
+
+SIM_CORES = 256
+KT = 2
+NW = 128 * KT
+NX = 256
+KA = 192
+KB = NW - KA
+FWD = 8
+SMALL = 4
+
+SCRATCH = {
+    "xt": ("sbuf", [128, 4 * NX * KT], "bfloat16"),
+    "xq": ("sbuf", [128, NX * KT], "float8_e4m3fn_x4"),
+    "xs": ("sbuf", [128, NX * KT], "uint8"),
+    "wq": ("sbuf", [128, NW], "float8_e4m3fn_x4"),
+    "wp": ("sbuf", [128, NW], "uint8"),
+    "dS": ("dram", [128, NW], "uint8"),
+    "dA": ("dram", [128, KA], "float8_e4m3fn_x4"),
+    "ps": ("psum", [128, 512], "float32"),
+    "yt": ("sbuf", [128, NX], "float32"),
+}
+if KB:
+    SCRATCH["dB"] = ("dram", [128, KB], "float8_e4m3fn_x4")
+
+SEMAPHORES = ["ldS", "ldA", "ldB", "inS", "inA", "inB", "okS", "okA", "okB", "sent",
+              "x0", "x1", "q0", "q1", "mm", "cp", "st"]
+
+
+def _place(topo, c):
+    return (topo.host(c), topo.chip(c))
+
+
+def _plan(T, topo):
+    ranks = list(T.cores)
+    root = ranks[T.root]
+    here = _place(topo, root)
+    home = [c for c in ranks if c != root and _place(topo, c) == here]
+    chips = {}
+    for c in ranks:
+        if _place(topo, c) != here:
+            chips.setdefault(_place(topo, c), []).append(c)
+    pairs = []
+    for where in sorted(chips):
+        group = chips[where]
+        same = [c for c in group if topo.die(c) == topo.die(root)]
+        near = (same or group)[0]
+        pairs.append((near, [c for c in group if c != near]))
+    a = [p for p in pairs if topo.same_plane(root, p[0])]
+    b = [p for p in pairs if not topo.same_plane(root, p[0])]
+    order = []
+    while a or b:
+        if a:
+            order.append(a.pop(0))
+        if b:
+            order.append(b.pop(0))
+    relays = {}
+    if KB:
+        other = [c for c in range(SIM_CORES) if _place(topo, c) == here and topo.die(c) != topo.die(root)]
+        for near, _ in order:
+            can = [c for c in other if topo.may_write(c, near)]
+            pick = [c for c in can if c in home] or [c for c in can if c not in ranks]
+            relays.setdefault(pick[0], []).append(near)
+    return root, home, order, relays
+
+
+def _engines(mask, n):
+    bits = [b for b in range(mask.bit_length()) if (mask >> b) & 1]
+    n = min(n, len(bits))
+    chosen = bits[::len(bits) // n][:n]
+    return sum(1 << b for b in chosen), n
+
+
+def _common(topo, core, dests):
+    m = topo.mask(core, dests[0])
+    for d in dests:
+        m &= topo.mask(core, d)
+    return m
+
+
+def rank_program(g, core, T, topo):
+    root, home, order, relays = _plan(T, topo)
+    rank = T.rank_of(core)
+    if rank is None and core not in relays:
+        return
+    s = T.sem
+    u8 = dt.uint8
+    nears = [p[0] for p in order]
+    fars = {p[0]: p[1] for p in order}
+    sent = [0]
+
+    def dA():
+        return T.dA[:].bitcast(u8)
+
+    def dB():
+        return T.dB[:].bitcast(u8)
+
+    def wqA():
+        return T.wq[:, 0:KA].bitcast(u8)
+
+    def wqB():
+        return T.wq[:, KA:NW].bitcast(u8)
+
+    def send(src, dst, dests, mask, n, rsem):
+        ids = []
+        for d in dests:
+            rid, pid = topo.addr(d, core)
+            ids.append(DstId(rid=rid, pnc=pid))
+        g.remote_dma_fused([RemoteDMATransfer(dst_ids=ids, dma_engine_mask=mask, remote_sem=rsem,
+                                              srcs=[src], dsts=[dst() for _ in dests], alu_op=0)], local_sem=s.sent)
+        sent[0] += n
+
+    def planes():
+        return T.wp[:]
+
+    def dSv():
+        return T.dS[:]
+
+    off_mask, off_n = _engines(_common(topo, root, nears), 16)
+    stay = _common(topo, root, home + list(relays)) & ~_common(topo, root, nears)
+    stay = stay or _common(topo, root, home + list(relays))
+    stay_mask, stay_n = _engines(stay, SMALL)
+    need = {"okS": 0, "okA": 0, "okB": 0}
+
+    if core == root:
+        if KB:
+            g.sync.dma_start(dB(), T.wc[:, 4 * KA:4 * NW]).then_inc(s.ldB, 16)
+        g.scalar.dma_start(T.dS[:], T.ws[:]).then_inc(s.ldS, 16)
+        g.sync.dma_start(dA(), T.wc[:, 0:4 * KA]).then_inc(s.ldA, 16)
+        g.scalar.dma_start(T.wp[:], T.ws[:]).then_inc(s.okS, 16)
+        g.sync.dma_start(T.wq[:].bitcast(u8), T.wc[:]).then_inc(s.okA, 16)
+        need["okS"] = 16
+        need["okA"] = 16
+    if rank is not None:
+        g.sync.dma_start(T.xt[:, 0:4 * NX], T.x[:, 0:4 * NX]).then_inc(s.x0, 16)
+        g.scalar.dma_start(T.xt[:, 4 * NX:8 * NX], T.x[:, 4 * NX:8 * NX]).then_inc(s.x1, 16)
+
+    if core == root:
+        if KB:
+            g.wait_ge(s.ldB, 16)
+            send(dB(), dB, sorted(set(home) | set(relays)), stay_mask, stay_n, s.inB)
+        g.wait_ge(s.ldS, 16)
+        send(T.dS[:], dSv, nears, off_mask, off_n, s.inS)
+        g.wait_ge(s.ldA, 16)
+        send(dA(), dA, nears, off_mask, off_n, s.inA)
+        if home:
+            send(T.dS[:], planes, home, stay_mask, stay_n, s.okS)
+            send(dA(), wqA, home, stay_mask, stay_n, s.okA)
+    if core in relays:
+        m, n = _engines(_common(topo, core, relays[core]), SMALL)
+        g.wait_ge(s.inB, stay_n)
+        send(dB(), dB, relays[core], m, n, s.inB)
+    if core in home:
+        need["okS"] = stay_n
+        need["okA"] = stay_n
+        if KB:
+            g.scalar.wait_ge(s.inB, stay_n)
+            g.scalar.dma_start(wqB(), dB()).then_inc(s.okB, 16)
+            need["okB"] = 16
+    if core in fars:
+        m, n = _engines(_common(topo, core, fars[core]), FWD)
+        g.wait_ge(s.inS, off_n)
+        send(T.dS[:], planes, fars[core], m, n, s.okS)
+        g.scalar.wait_ge(s.inS, off_n)
+        g.scalar.dma_start(T.wp[:], T.dS[:]).then_inc(s.okS, 16)
+        g.wait_ge(s.inA, off_n)
+        send(dA(), wqA, fars[core], m, n, s.okA)
+        g.sync.wait_ge(s.inA, off_n)
+        g.sync.dma_start(wqA(), dA()).then_inc(s.okA, 16)
+        need["okS"] = 16
+        need["okA"] = 16
+        if KB:
+            rel = [r for r in relays if core in relays[r]][0]
+            nb = _engines(_common(topo, rel, relays[rel]), SMALL)[1]
+            g.wait_ge(s.inB, nb)
+            send(dB(), wqB, fars[core], m, n, s.okB)
+            g.scalar.wait_ge(s.inB, nb)
+            g.scalar.dma_start(wqB(), dB()).then_inc(s.okB, 16)
+            need["okB"] = 16
+    for near in fars:
+        if core in fars[near]:
+            n = _engines(_common(topo, near, fars[near]), FWD)[1]
+            need["okS"] = n
+            need["okA"] = n
+            need["okB"] = n if KB else 0
+    if sent[0]:
+        g.wait_ge(s.sent, sent[0])
+    if rank is None:
+        return
+
+    v, te = g.vector, g.tensor
+    v.wait_ge(s.x0, 16)
+    v.quantize_mx(T.xq[:, 0:NX], T.xs[:, 0:NX], T.xt[:, 0:4 * NX]).then_inc(s.q0, 1)
+    v.wait_ge(s.x1, 16)
+    v.quantize_mx(T.xq[:, NX:2 * NX], T.xs[:, NX:2 * NX], T.xt[:, 4 * NX:8 * NX]).then_inc(s.q1, 1)
+
+    te.wait_ge(s.q0, 1)
+    te.wait_ge(s.q1, 1)
+    te.wait_ge(s.okS, need["okS"])
+    te.wait_ge(s.okA, need["okA"])
+    te.matmul_mx(T.ps[:, 0:NX], T.wq[:, 0:128], T.wp[:, 0:128], T.xq[:, 0:NX], T.xs[:, 0:NX], True, False)
+    if need["okB"]:
+        te.wait_ge(s.okB, need["okB"])
+    te.matmul_mx(T.ps[:, 0:NX], T.wq[:, 128:256], T.wp[:, 128:256], T.xq[:, NX:2 * NX], T.xs[:, NX:2 * NX],
+                 False, True).then_inc(s.mm, 1)
+
+    v.wait_ge(s.mm, 1)
+    v.tensor_copy(T.yt[:], T.ps[:, 0:NX]).then_inc(s.cp, 1)
+    g.sync.wait_ge(s.cp, 1)
+    g.sync.dma_start(T.y[:], T.yt[:]).then_inc(s.st, 16)
+    g.sync.wait_ge(s.st, 16)

@@ -5,9 +5,8 @@ SIM_CORES = 256
 KT = 2
 NW = 128 * KT
 NX = 256
+K0 = 128
 KA = 192
-KB = NW - KA
-FWD = 8
 SMALL = 4
 
 SCRATCH = {
@@ -17,14 +16,14 @@ SCRATCH = {
     "wq": ("sbuf", [128, NW], "float8_e4m3fn_x4"),
     "wp": ("sbuf", [128, NW], "uint8"),
     "dS": ("dram", [128, NW], "uint8"),
-    "dA": ("dram", [128, KA], "float8_e4m3fn_x4"),
+    "dA": ("dram", [128, K0], "float8_e4m3fn_x4"),
+    "dC": ("dram", [128, KA - K0], "float8_e4m3fn_x4"),
+    "dB": ("dram", [128, NW - KA], "float8_e4m3fn_x4"),
     "ps": ("psum", [128, 512], "float32"),
     "yt": ("sbuf", [128, NX], "float32"),
 }
-if KB:
-    SCRATCH["dB"] = ("dram", [128, KB], "float8_e4m3fn_x4")
 
-SEMAPHORES = ["ldS", "ldA", "ldB", "inS", "inA", "inB", "okS", "okA", "okB", "sent",
+SEMAPHORES = ["ldS", "ldA", "ldC", "ldB", "inS", "inA", "inC", "inB", "okS", "okA", "okT", "sent",
               "x0", "x1", "q0", "q1", "mm", "cp", "st"]
 
 
@@ -41,34 +40,25 @@ def _plan(T, topo):
     for c in ranks:
         if _place(topo, c) != here:
             chips.setdefault(_place(topo, c), []).append(c)
-    pairs = []
+    fars = {}
     for where in sorted(chips):
         group = chips[where]
         same = [c for c in group if topo.die(c) == topo.die(root)]
         near = (same or group)[0]
-        pairs.append((near, [c for c in group if c != near]))
-    a = [p for p in pairs if topo.same_plane(root, p[0])]
-    b = [p for p in pairs if not topo.same_plane(root, p[0])]
-    order = []
-    while a or b:
-        if a:
-            order.append(a.pop(0))
-        if b:
-            order.append(b.pop(0))
+        fars[near] = [c for c in group if c != near]
+    other = [c for c in range(SIM_CORES) if _place(topo, c) == here and topo.die(c) != topo.die(root)]
     relays = {}
-    if KB:
-        other = [c for c in range(SIM_CORES) if _place(topo, c) == here and topo.die(c) != topo.die(root)]
-        for near, _ in order:
-            can = [c for c in other if topo.may_write(c, near)]
-            pick = [c for c in can if c in home] or [c for c in can if c not in ranks]
-            relays.setdefault(pick[0], []).append(near)
-    return root, home, order, relays
+    for near in fars:
+        can = [c for c in other if topo.may_write(c, near)]
+        pick = [c for c in can if c in home] or [c for c in can if c not in ranks]
+        relays.setdefault(pick[0], []).append(near)
+    return root, home, fars, relays
 
 
-def _engines(mask, n):
+def _engines(mask, n, first=0):
     bits = [b for b in range(mask.bit_length()) if (mask >> b) & 1]
     n = min(n, len(bits))
-    chosen = bits[::len(bits) // n][:n]
+    chosen = bits[first::len(bits) // n][:n]
     return sum(1 << b for b in chosen), n
 
 
@@ -80,56 +70,61 @@ def _common(topo, core, dests):
 
 
 def rank_program(g, core, T, topo):
-    root, home, order, relays = _plan(T, topo)
+    root, home, fars, relays = _plan(T, topo)
     rank = T.rank_of(core)
     if rank is None and core not in relays:
         return
     s = T.sem
     u8 = dt.uint8
-    nears = [p[0] for p in order]
-    fars = {p[0]: p[1] for p in order}
+    nears = list(fars)
     sent = [0]
+
+    def dS():
+        return T.dS[:]
 
     def dA():
         return T.dA[:].bitcast(u8)
 
+    def dC():
+        return T.dC[:].bitcast(u8)
+
     def dB():
         return T.dB[:].bitcast(u8)
 
-    def wqA():
-        return T.wq[:, 0:KA].bitcast(u8)
-
-    def wqB():
-        return T.wq[:, KA:NW].bitcast(u8)
-
-    def send(src, dst, dests, mask, n, rsem):
-        ids = []
-        for d in dests:
-            rid, pid = topo.addr(d, core)
-            ids.append(DstId(rid=rid, pnc=pid))
-        g.remote_dma_fused([RemoteDMATransfer(dst_ids=ids, dma_engine_mask=mask, remote_sem=rsem,
-                                              srcs=[src], dsts=[dst() for _ in dests], alu_op=0)], local_sem=s.sent)
-        sent[0] += n
-
-    def planes():
+    def wp():
         return T.wp[:]
 
-    def dSv():
-        return T.dS[:]
+    def wq(a, b):
+        return lambda: T.wq[:, a:b].bitcast(u8)
 
-    off_mask, off_n = _engines(_common(topo, root, nears), 16)
-    stay = _common(topo, root, home + list(relays)) & ~_common(topo, root, nears)
-    stay = stay or _common(topo, root, home + list(relays))
+    def call(parts):
+        trs = []
+        for src, dst, dests, mask, n, rsem in parts:
+            ids = []
+            for d in dests:
+                rid, pid = topo.addr(d, core)
+                ids.append(DstId(rid=rid, pnc=pid))
+            trs.append(RemoteDMATransfer(dst_ids=ids, dma_engine_mask=mask, remote_sem=rsem,
+                                         srcs=[src()], dsts=[dst() for _ in dests], alu_op=0))
+            sent[0] += n
+        g.remote_dma_fused(trs, local_sem=s.sent)
+
+    leave = _common(topo, root, nears)
+    planes = [[c for c in nears if topo.same_plane(root, c)], [c for c in nears if not topo.same_plane(root, c)]]
+    off = [(grp,) + _engines(leave, SMALL, k) for k, grp in enumerate(planes) if grp]
+    off_n = off[0][2]
+    inside = sorted(set(home) | set(relays))
+    stay = (_common(topo, root, inside) & ~leave) or _common(topo, root, inside)
     stay_mask, stay_n = _engines(stay, SMALL)
-    need = {"okS": 0, "okA": 0, "okB": 0}
+    need = {"okS": 0, "okA": 0, "okT": 0}
 
     if core == root:
-        if KB:
-            g.sync.dma_start(dB(), T.wc[:, 4 * KA:4 * NW]).then_inc(s.ldB, 16)
-        g.scalar.dma_start(T.dS[:], T.ws[:]).then_inc(s.ldS, 16)
-        g.sync.dma_start(dA(), T.wc[:, 0:4 * KA]).then_inc(s.ldA, 16)
-        g.scalar.dma_start(T.wp[:], T.ws[:]).then_inc(s.okS, 16)
-        g.sync.dma_start(T.wq[:].bitcast(u8), T.wc[:]).then_inc(s.okA, 16)
+        g.sync.dma_start(dB(), T.wc[:, 4 * KA:4 * NW]).then_inc(s.ldB, 16)
+        g.scalar.dma_start(dS(), T.ws[:]).then_inc(s.ldS, 16)
+        g.sync.dma_start(dA(), T.wc[:, 0:4 * K0]).then_inc(s.ldA, 16)
+        g.scalar.dma_start(dC(), T.wc[:, 4 * K0:4 * KA]).then_inc(s.ldC, 16)
+        g.scalar.dma_start(wp(), T.ws[:]).then_inc(s.okS, 16)
+        g.sync.dma_start(wq(0, NW)(), T.wc[:]).then_inc(s.okA, 16)
         need["okS"] = 16
         need["okA"] = 16
     if rank is not None:
@@ -137,53 +132,60 @@ def rank_program(g, core, T, topo):
         g.scalar.dma_start(T.xt[:, 4 * NX:8 * NX], T.x[:, 4 * NX:8 * NX]).then_inc(s.x1, 16)
 
     if core == root:
-        if KB:
-            g.wait_ge(s.ldB, 16)
-            send(dB(), dB, sorted(set(home) | set(relays)), stay_mask, stay_n, s.inB)
+        g.wait_ge(s.ldB, 16)
+        call([(dB, dB, inside, stay_mask, stay_n, s.inB)])
         g.wait_ge(s.ldS, 16)
-        send(T.dS[:], dSv, nears, off_mask, off_n, s.inS)
+        call([(dS, dS, grp, m, n, s.inS) for grp, m, n in off])
         g.wait_ge(s.ldA, 16)
-        send(dA(), dA, nears, off_mask, off_n, s.inA)
+        call([(dA, dA, grp, m, n, s.inA) for grp, m, n in off])
+        g.wait_ge(s.ldC, 16)
+        call([(dC, dC, grp, m, n, s.inC) for grp, m, n in off])
         if home:
-            send(T.dS[:], planes, home, stay_mask, stay_n, s.okS)
-            send(dA(), wqA, home, stay_mask, stay_n, s.okA)
+            g.wait_ge(s.okS, 16)
+            call([(wp, wp, home, stay_mask, stay_n, s.okS)])
+            g.wait_ge(s.okA, 16)
+            call([(wq(0, KA), wq(0, KA), home, stay_mask, stay_n, s.okA)])
     if core in relays:
         m, n = _engines(_common(topo, core, relays[core]), SMALL)
         g.wait_ge(s.inB, stay_n)
-        send(dB(), dB, relays[core], m, n, s.inB)
+        call([(dB, dB, relays[core], m, n, s.inB)])
     if core in home:
         need["okS"] = stay_n
         need["okA"] = stay_n
-        if KB:
-            g.scalar.wait_ge(s.inB, stay_n)
-            g.scalar.dma_start(wqB(), dB()).then_inc(s.okB, 16)
-            need["okB"] = 16
+        g.scalar.wait_ge(s.inB, stay_n)
+        g.scalar.dma_start(wq(KA, NW)(), dB()).then_inc(s.okT, 16)
+        need["okT"] = 16
     if core in fars:
-        m, n = _engines(_common(topo, core, fars[core]), FWD)
+        every = _common(topo, core, fars[core])
+        m, n = _engines(every, 16)
+        half = [_engines(every, n // 2, k) for k in range(2)]
+        rel = [r for r in relays if core in relays[r]][0]
+        nb = _engines(_common(topo, rel, relays[rel]), SMALL)[1]
         g.wait_ge(s.inS, off_n)
-        send(T.dS[:], planes, fars[core], m, n, s.okS)
-        g.scalar.wait_ge(s.inS, off_n)
-        g.scalar.dma_start(T.wp[:], T.dS[:]).then_inc(s.okS, 16)
+        call([(dS, wp, fars[core], m, n, s.okS)])
         g.wait_ge(s.inA, off_n)
-        send(dA(), wqA, fars[core], m, n, s.okA)
+        call([(dA, wq(0, K0), fars[core], m, n, s.okA)])
+        g.wait_ge(s.inC, off_n)
+        g.wait_ge(s.inB, nb)
+        call([(dC, wq(K0, KA), fars[core], half[0][0], half[0][1], s.okT),
+              (dB, wq(KA, NW), fars[core], half[1][0], half[1][1], s.okT)])
+        g.scalar.wait_ge(s.inS, off_n)
+        g.scalar.dma_start(wp(), dS()).then_inc(s.okS, 16)
         g.sync.wait_ge(s.inA, off_n)
-        g.sync.dma_start(wqA(), dA()).then_inc(s.okA, 16)
+        g.sync.dma_start(wq(0, K0)(), dA()).then_inc(s.okA, 16)
+        g.sync.wait_ge(s.inC, off_n)
+        g.sync.dma_start(wq(K0, KA)(), dC()).then_inc(s.okT, 16)
+        g.scalar.wait_ge(s.inB, nb)
+        g.scalar.dma_start(wq(KA, NW)(), dB()).then_inc(s.okT, 16)
         need["okS"] = 16
         need["okA"] = 16
-        if KB:
-            rel = [r for r in relays if core in relays[r]][0]
-            nb = _engines(_common(topo, rel, relays[rel]), SMALL)[1]
-            g.wait_ge(s.inB, nb)
-            send(dB(), wqB, fars[core], m, n, s.okB)
-            g.scalar.wait_ge(s.inB, nb)
-            g.scalar.dma_start(wqB(), dB()).then_inc(s.okB, 16)
-            need["okB"] = 16
+        need["okT"] = 32
     for near in fars:
         if core in fars[near]:
-            n = _engines(_common(topo, near, fars[near]), FWD)[1]
+            n = _engines(_common(topo, near, fars[near]), 16)[1]
             need["okS"] = n
             need["okA"] = n
-            need["okB"] = n if KB else 0
+            need["okT"] = 2 * (n // 2)
     if sent[0]:
         g.wait_ge(s.sent, sent[0])
     if rank is None:
@@ -200,8 +202,8 @@ def rank_program(g, core, T, topo):
     te.wait_ge(s.okS, need["okS"])
     te.wait_ge(s.okA, need["okA"])
     te.matmul_mx(T.ps[:, 0:NX], T.wq[:, 0:128], T.wp[:, 0:128], T.xq[:, 0:NX], T.xs[:, 0:NX], True, False)
-    if need["okB"]:
-        te.wait_ge(s.okB, need["okB"])
+    if need["okT"]:
+        te.wait_ge(s.okT, need["okT"])
     te.matmul_mx(T.ps[:, 0:NX], T.wq[:, 128:256], T.wp[:, 128:256], T.xq[:, NX:2 * NX], T.xs[:, NX:2 * NX],
                  False, True).then_inc(s.mm, 1)
 

@@ -5,9 +5,13 @@ SIM_CORES = 256
 KT = 2
 NW = 128 * KT
 NX = 256
-K0 = 128
-KA = 192
+Q = NW // 4
 SMALL = 4
+
+PIECES = {"S0": (False, 0, 128), "S1": (False, 128, 256),
+          "A0": (True, 0, Q), "A1": (True, Q, 2 * Q), "C": (True, 2 * Q, 3 * Q), "B": (True, 3 * Q, 4 * Q)}
+FIRST = ("S0", "A0", "A1")
+NEAR, FAR = ("S0", "A0", "C"), ("S1", "A1", "B")
 
 SCRATCH = {
     "xt": ("sbuf", [128, 4 * NX * KT], "bfloat16"),
@@ -15,15 +19,17 @@ SCRATCH = {
     "xs": ("sbuf", [128, NX * KT], "uint8"),
     "wq": ("sbuf", [128, NW], "float8_e4m3fn_x4"),
     "wp": ("sbuf", [128, NW], "uint8"),
-    "dS": ("dram", [128, NW], "uint8"),
-    "dA": ("dram", [128, K0], "float8_e4m3fn_x4"),
-    "dC": ("dram", [128, KA - K0], "float8_e4m3fn_x4"),
-    "dB": ("dram", [128, NW - KA], "float8_e4m3fn_x4"),
+    "dS0": ("dram", [128, 128], "uint8"),
+    "dS1": ("dram", [128, 128], "uint8"),
+    "dA0": ("dram", [128, Q], "float8_e4m3fn_x4"),
+    "dA1": ("dram", [128, Q], "float8_e4m3fn_x4"),
+    "dC": ("dram", [128, Q], "float8_e4m3fn_x4"),
+    "dB": ("dram", [128, Q], "float8_e4m3fn_x4"),
     "ps": ("psum", [128, 512], "float32"),
     "yt": ("sbuf", [128, NX], "float32"),
 }
 
-SEMAPHORES = ["ldS", "ldA", "ldC", "ldB", "inS", "inA", "inC", "inB", "okS", "okA", "okT", "sent",
+SEMAPHORES = ["ldS", "ldA", "ldC", "ldB", "inS", "inA", "inT", "ok0", "ok1", "sent",
               "x0", "x1", "q0", "q1", "mm", "cp", "st"]
 
 
@@ -40,19 +46,27 @@ def _plan(T, topo):
     for c in ranks:
         if _place(topo, c) != here:
             chips.setdefault(_place(topo, c), []).append(c)
-    fars = {}
+    sites = []
     for where in sorted(chips):
         group = chips[where]
-        same = [c for c in group if topo.die(c) == topo.die(root)]
-        near = (same or group)[0]
-        fars[near] = [c for c in group if c != near]
-    other = [c for c in range(SIM_CORES) if _place(topo, c) == here and topo.die(c) != topo.die(root)]
+        near = [c for c in group if topo.die(c) == topo.die(root)][0]
+        far = [c for c in group if c != near][0]
+        sites.append((near, far))
+    planes = [[p for p in sites if topo.same_plane(root, p[0])], [p for p in sites if not topo.same_plane(root, p[0])]]
+    planes = [grp for grp in planes if grp]
+    everyone = [c for p in sites for c in p]
+    free = [c for c in range(SIM_CORES) if _place(topo, c) == here and c not in ranks]
+    free.sort(key=lambda c: (sum(1 for d in everyone if topo.may_write(c, d)), c))
     relays = {}
-    for near in fars:
-        can = [c for c in other if topo.may_write(c, near)]
-        pick = [c for c in can if c in home] or [c for c in can if c not in ranks]
-        relays.setdefault(pick[0], []).append(near)
-    return root, home, fars, relays
+    for piece, side, same_die in (("B", 1, False), ("C", 0, True)):
+        relays[piece] = {}
+        for k, grp in enumerate(planes):
+            dests = [p[side] for p in grp]
+            pick = [c for c in free if (topo.die(c) == topo.die(root)) == same_die
+                    and all(topo.may_write(c, d) for d in dests)][0]
+            free.remove(pick)
+            relays[piece][pick] = dests
+    return root, home, sites, planes, relays
 
 
 def _engines(mask, n, first=0):
@@ -69,33 +83,34 @@ def _common(topo, core, dests):
     return m
 
 
+def _turn(seq, k):
+    k %= len(seq)
+    return list(seq[k:]) + list(seq[:k])
+
+
 def rank_program(g, core, T, topo):
-    root, home, fars, relays = _plan(T, topo)
+    root, home, sites, planes, relays = _plan(T, topo)
     rank = T.rank_of(core)
-    if rank is None and core not in relays:
+    helpers = [c for piece in relays for c in relays[piece]]
+    if rank is None and core not in helpers:
         return
     s = T.sem
     u8 = dt.uint8
-    nears = list(fars)
     sent = [0]
 
-    def dS():
-        return T.dS[:]
+    def dram(p):
+        return (lambda: T["d" + p][:].bitcast(u8)) if PIECES[p][0] else (lambda: T["d" + p][:])
 
-    def dA():
-        return T.dA[:].bitcast(u8)
+    def sbuf(p):
+        codes, a, b = PIECES[p]
+        return (lambda: T.wq[:, a:b].bitcast(u8)) if codes else (lambda: T.wp[:, a:b])
 
-    def dC():
-        return T.dC[:].bitcast(u8)
+    def given(p):
+        codes, a, b = PIECES[p]
+        return T.wc[:, 4 * a:4 * b] if codes else T.ws[:, a:b]
 
-    def dB():
-        return T.dB[:].bitcast(u8)
-
-    def wp():
-        return T.wp[:]
-
-    def wq(a, b):
-        return lambda: T.wq[:, a:b].bitcast(u8)
+    def ok(p):
+        return s.ok0 if p in FIRST else s.ok1
 
     def call(parts):
         trs = []
@@ -109,83 +124,74 @@ def rank_program(g, core, T, topo):
             sent[0] += n
         g.remote_dma_fused(trs, local_sem=s.sent)
 
-    leave = _common(topo, root, nears)
-    planes = [[c for c in nears if topo.same_plane(root, c)], [c for c in nears if not topo.same_plane(root, c)]]
-    off = [(grp,) + _engines(leave, SMALL, k) for k, grp in enumerate(planes) if grp]
-    off_n = off[0][2]
-    inside = sorted(set(home) | set(relays))
+    everyone = [c for p in sites for c in p]
+    leave = _common(topo, root, everyone)
+    ways = [(side, grp) for side in (0, 1) for grp in planes]
+    share = 1
+    while share * 2 * len(ways) <= bin(leave).count("1"):
+        share *= 2
+    off = [(side, _turn([p[side] for p in grp], side)) + _engines(leave, share, k)
+           for k, (side, grp) in enumerate(ways)]
+    inside = sorted(set(home) | set(helpers))
     stay = (_common(topo, root, inside) & ~leave) or _common(topo, root, inside)
-    stay_mask, stay_n = _engines(stay, SMALL)
-    need = {"okS": 0, "okA": 0, "okT": 0}
+    hand = {piece: _engines(stay, SMALL, k) for k, piece in enumerate(relays)}
+    home_mask, home_n = _engines(stay, 2 * SMALL)
+    need = [0, 0]
 
     if core == root:
-        g.sync.dma_start(dB(), T.wc[:, 4 * KA:4 * NW]).then_inc(s.ldB, 16)
-        g.scalar.dma_start(dS(), T.ws[:]).then_inc(s.ldS, 16)
-        g.sync.dma_start(dA(), T.wc[:, 0:4 * K0]).then_inc(s.ldA, 16)
-        g.scalar.dma_start(dC(), T.wc[:, 4 * K0:4 * KA]).then_inc(s.ldC, 16)
-        g.scalar.dma_start(wp(), T.ws[:]).then_inc(s.okS, 16)
-        g.sync.dma_start(wq(0, NW)(), T.wc[:]).then_inc(s.okA, 16)
-        need["okS"] = 16
-        need["okA"] = 16
+        g.sync.dma_start(dram("B")(), given("B")).then_inc(s.ldB, 16)
+        g.scalar.dma_start(dram("C")(), given("C")).then_inc(s.ldC, 16)
+        g.sync.dma_start(dram("S0")(), given("S0")).then_inc(s.ldS, 16)
+        g.scalar.dma_start(dram("S1")(), given("S1")).then_inc(s.ldS, 16)
+        g.sync.dma_start(dram("A0")(), given("A0")).then_inc(s.ldA, 16)
+        g.scalar.dma_start(dram("A1")(), given("A1")).then_inc(s.ldA, 16)
+        g.scalar.dma_start(T.wp[:], T.ws[:]).then_inc(s.ok0, 16)
+        g.sync.dma_start(T.wq[:].bitcast(u8), T.wc[:]).then_inc(s.ok0, 16)
+        need[0] = 32
     if rank is not None:
         g.sync.dma_start(T.xt[:, 0:4 * NX], T.x[:, 0:4 * NX]).then_inc(s.x0, 16)
         g.scalar.dma_start(T.xt[:, 4 * NX:8 * NX], T.x[:, 4 * NX:8 * NX]).then_inc(s.x1, 16)
 
     if core == root:
-        g.wait_ge(s.ldB, 16)
-        call([(dB, dB, inside, stay_mask, stay_n, s.inB)])
-        g.wait_ge(s.ldS, 16)
-        call([(dS, dS, grp, m, n, s.inS) for grp, m, n in off])
-        g.wait_ge(s.ldA, 16)
-        call([(dA, dA, grp, m, n, s.inA) for grp, m, n in off])
-        g.wait_ge(s.ldC, 16)
-        call([(dC, dC, grp, m, n, s.inC) for grp, m, n in off])
+        for p, ld in (("B", s.ldB), ("C", s.ldC)):
+            g.wait_ge(ld, 16)
+            call([(dram(p), dram(p), list(relays[p]), hand[p][0], hand[p][1], s.inT)])
+        for k, (ld, rsem) in enumerate(((s.ldS, s.inS), (s.ldA, s.inA))):
+            g.wait_ge(ld, 32)
+            call([(dram((NEAR, FAR)[side][k]), dram((NEAR, FAR)[side][k]), dests, m, n, rsem)
+                  for side, dests, m, n in off])
         if home:
-            g.wait_ge(s.okS, 16)
-            call([(wp, wp, home, stay_mask, stay_n, s.okS)])
-            g.wait_ge(s.okA, 16)
-            call([(wq(0, KA), wq(0, KA), home, stay_mask, stay_n, s.okA)])
-    if core in relays:
-        m, n = _engines(_common(topo, core, relays[core]), SMALL)
-        g.wait_ge(s.inB, stay_n)
-        call([(dB, dB, relays[core], m, n, s.inB)])
+            g.wait_ge(s.ok0, 32)
+            call([(lambda: T.wp[:], lambda: T.wp[:], home, home_mask, home_n, s.ok0)])
+            call([(lambda: T.wq[:].bitcast(u8), lambda: T.wq[:].bitcast(u8), home, home_mask, home_n, s.ok0)])
+    for p in relays:
+        if core in relays[p]:
+            dests = relays[p][core]
+            m, n = _engines(_common(topo, core, dests), SMALL)
+            g.wait_ge(s.inT, hand[p][1])
+            call([(dram(p), dram(p), _turn(dests, 2), m, n, s.inT)])
     if core in home:
-        need["okS"] = stay_n
-        need["okA"] = stay_n
-        g.scalar.wait_ge(s.inB, stay_n)
-        g.scalar.dma_start(wq(KA, NW)(), dB()).then_inc(s.okT, 16)
-        need["okT"] = 16
-    if core in fars:
-        every = _common(topo, core, fars[core])
-        m, n = _engines(every, 16)
-        half = [_engines(every, n // 2, k) for k in range(2)]
-        rel = [r for r in relays if core in relays[r]][0]
-        nb = _engines(_common(topo, rel, relays[rel]), SMALL)[1]
-        g.wait_ge(s.inS, off_n)
-        call([(dS, wp, fars[core], m, n, s.okS)])
-        g.wait_ge(s.inA, off_n)
-        call([(dA, wq(0, K0), fars[core], m, n, s.okA)])
-        g.wait_ge(s.inC, off_n)
-        g.wait_ge(s.inB, nb)
-        call([(dC, wq(K0, KA), fars[core], half[0][0], half[0][1], s.okT),
-              (dB, wq(KA, NW), fars[core], half[1][0], half[1][1], s.okT)])
-        g.scalar.wait_ge(s.inS, off_n)
-        g.scalar.dma_start(wp(), dS()).then_inc(s.okS, 16)
-        g.sync.wait_ge(s.inA, off_n)
-        g.sync.dma_start(wq(0, K0)(), dA()).then_inc(s.okA, 16)
-        g.sync.wait_ge(s.inC, off_n)
-        g.sync.dma_start(wq(K0, KA)(), dC()).then_inc(s.okT, 16)
-        g.scalar.wait_ge(s.inB, nb)
-        g.scalar.dma_start(wq(KA, NW)(), dB()).then_inc(s.okT, 16)
-        need["okS"] = 16
-        need["okA"] = 16
-        need["okT"] = 32
-    for near in fars:
-        if core in fars[near]:
-            n = _engines(_common(topo, near, fars[near]), 16)[1]
-            need["okS"] = n
-            need["okA"] = n
-            need["okT"] = 2 * (n // 2)
+        need[0] = 2 * home_n
+    for pair in sites:
+        if core in pair:
+            side = pair.index(core)
+            mate = pair[1 - side]
+            mine = (NEAR, FAR)[side]
+            m, n = _engines(topo.mask(core, mate), 16)
+            last = [c for c in relays[mine[2]] if core in relays[mine[2]][c]][0]
+            counts = (share, share, _engines(_common(topo, last, relays[mine[2]][last]), SMALL)[1])
+            sems = (s.inS, s.inA, s.inT)
+            for p, sem, cnt in zip(mine, sems, counts):
+                g.wait_ge(sem, cnt)
+                call([(dram(p), sbuf(p), [mate], m, n, ok(p))])
+            for p, sem, cnt, q in zip(mine, sems, counts, (g.scalar, g.sync, g.scalar)):
+                q.wait_ge(sem, cnt)
+                q.dma_start(sbuf(p)(), dram(p)()).then_inc(ok(p), 16)
+            n_back = _engines(topo.mask(mate, core), 16)[1]
+            theirs = (NEAR, FAR)[1 - side]
+            for k in (0, 1):
+                need[k] = sum(16 for p in mine if (p in FIRST) == (k == 0)) \
+                    + sum(n_back for p in theirs if (p in FIRST) == (k == 0))
     if sent[0]:
         g.wait_ge(s.sent, sent[0])
     if rank is None:
@@ -199,11 +205,10 @@ def rank_program(g, core, T, topo):
 
     te.wait_ge(s.q0, 1)
     te.wait_ge(s.q1, 1)
-    te.wait_ge(s.okS, need["okS"])
-    te.wait_ge(s.okA, need["okA"])
+    te.wait_ge(s.ok0, need[0])
     te.matmul_mx(T.ps[:, 0:NX], T.wq[:, 0:128], T.wp[:, 0:128], T.xq[:, 0:NX], T.xs[:, 0:NX], True, False)
-    if need["okT"]:
-        te.wait_ge(s.okT, need["okT"])
+    if need[1]:
+        te.wait_ge(s.ok1, need[1])
     te.matmul_mx(T.ps[:, 0:NX], T.wq[:, 128:256], T.wp[:, 128:256], T.xq[:, NX:2 * NX], T.xs[:, NX:2 * NX],
                  False, True).then_inc(s.mm, 1)
 

from concourse.bass import DstId, RemoteDMATransfer
from concourse.mybir import dt

SIM_CORES = 256
KT = 2
NW = 128 * KT
NX = 256
Q = NW // 4
SMALL = 4

PIECES = {"S0": (False, 0, 128), "S1": (False, 128, 256),
          "A0": (True, 0, Q), "A1": (True, Q, 2 * Q), "C": (True, 2 * Q, 3 * Q), "B": (True, 3 * Q, 4 * Q)}
FIRST = ("S0", "A0", "A1")
NEAR, FAR = ("S0", "A0", "C"), ("S1", "A1", "B")

SCRATCH = {
    "xt": ("sbuf", [128, 4 * NX * KT], "bfloat16"),
    "xq": ("sbuf", [128, NX * KT], "float8_e4m3fn_x4"),
    "xs": ("sbuf", [128, NX * KT], "uint8"),
    "wq": ("sbuf", [128, NW], "float8_e4m3fn_x4"),
    "wp": ("sbuf", [128, NW], "uint8"),
    "dS0": ("dram", [128, 128], "uint8"),
    "dS1": ("dram", [128, 128], "uint8"),
    "dA0": ("dram", [128, Q], "float8_e4m3fn_x4"),
    "dA1": ("dram", [128, Q], "float8_e4m3fn_x4"),
    "dC": ("dram", [128, Q], "float8_e4m3fn_x4"),
    "dB": ("dram", [128, Q], "float8_e4m3fn_x4"),
    "ps": ("psum", [128, 512], "float32"),
    "yt": ("sbuf", [128, NX], "float32"),
}

SEMAPHORES = ["ldS", "ldA", "ldC", "ldB", "inS", "inA", "inT", "ok0", "ok1", "sent",
              "x0", "x1", "q0", "q1", "mm", "cp", "st"]


def _place(topo, c):
    return (topo.host(c), topo.chip(c))


def _plan(T, topo):
    ranks = list(T.cores)
    root = ranks[T.root]
    here = _place(topo, root)
    home = [c for c in ranks if c != root and _place(topo, c) == here]
    chips = {}
    for c in ranks:
        if _place(topo, c) != here:
            chips.setdefault(_place(topo, c), []).append(c)
    sites = []
    for where in sorted(chips):
        group = chips[where]
        near = [c for c in group if topo.die(c) == topo.die(root)][0]
        far = [c for c in group if c != near][0]
        sites.append((near, far))
    planes = [[p for p in sites if topo.same_plane(root, p[0])], [p for p in sites if not topo.same_plane(root, p[0])]]
    planes = [grp for grp in planes if grp]
    everyone = [c for p in sites for c in p]
    free = [c for c in range(SIM_CORES) if _place(topo, c) == here and c not in ranks]
    free.sort(key=lambda c: (sum(1 for d in everyone if topo.may_write(c, d)), c))
    relays = {}
    for piece, side, same_die in (("B", 1, False), ("C", 0, True)):
        relays[piece] = {}
        for k, grp in enumerate(planes):
            dests = [p[side] for p in grp]
            pick = [c for c in free if (topo.die(c) == topo.die(root)) == same_die
                    and all(topo.may_write(c, d) for d in dests)][0]
            free.remove(pick)
            relays[piece][pick] = dests
    return root, home, sites, planes, relays


def _engines(mask, n, first=0):
    bits = [b for b in range(mask.bit_length()) if (mask >> b) & 1]
    n = min(n, len(bits))
    chosen = bits[first::len(bits) // n][:n]
    return sum(1 << b for b in chosen), n


def _common(topo, core, dests):
    m = topo.mask(core, dests[0])
    for d in dests:
        m &= topo.mask(core, d)
    return m


def _turn(seq, k):
    k %= len(seq)
    return list(seq[k:]) + list(seq[:k])


def rank_program(g, core, T, topo):
    root, home, sites, planes, relays = _plan(T, topo)
    rank = T.rank_of(core)
    helpers = [c for piece in relays for c in relays[piece]]
    if rank is None and core not in helpers:
        return
    s = T.sem
    u8 = dt.uint8
    sent = [0]

    def dram(p):
        return (lambda: T["d" + p][:].bitcast(u8)) if PIECES[p][0] else (lambda: T["d" + p][:])

    def sbuf(p):
        codes, a, b = PIECES[p]
        return (lambda: T.wq[:, a:b].bitcast(u8)) if codes else (lambda: T.wp[:, a:b])

    def given(p):
        codes, a, b = PIECES[p]
        return T.wc[:, 4 * a:4 * b] if codes else T.ws[:, a:b]

    def ok(p):
        return s.ok0 if p in FIRST else s.ok1

    def call(parts):
        trs = []
        for src, dst, dests, mask, n, rsem in parts:
            ids = []
            for d in dests:
                rid, pid = topo.addr(d, core)
                ids.append(DstId(rid=rid, pnc=pid))
            trs.append(RemoteDMATransfer(dst_ids=ids, dma_engine_mask=mask, remote_sem=rsem,
                                         srcs=[src()], dsts=[dst() for _ in dests], alu_op=0))
            sent[0] += n
        g.remote_dma_fused(trs, local_sem=s.sent)

    everyone = [c for p in sites for c in p]
    leave = _common(topo, root, everyone)
    ways = [(side, grp) for side in (0, 1) for grp in planes]
    share = 1
    while share * 2 * len(ways) <= bin(leave).count("1"):
        share *= 2
    off = [(side, _turn([p[side] for p in grp], side)) + _engines(leave, share, k)
           for k, (side, grp) in enumerate(ways)]
    inside = sorted(set(home) | set(helpers))
    stay = (_common(topo, root, inside) & ~leave) or _common(topo, root, inside)
    hand = {piece: _engines(stay, SMALL, k) for k, piece in enumerate(relays)}
    home_mask, home_n = _engines(stay, 2 * SMALL)
    need = [0, 0]

    if core == root:
        g.sync.dma_start(dram("B")(), given("B")).then_inc(s.ldB, 16)
        g.scalar.dma_start(dram("C")(), given("C")).then_inc(s.ldC, 16)
        g.sync.dma_start(dram("S0")(), given("S0")).then_inc(s.ldS, 16)
        g.scalar.dma_start(dram("S1")(), given("S1")).then_inc(s.ldS, 16)
        g.sync.dma_start(dram("A0")(), given("A0")).then_inc(s.ldA, 16)
        g.scalar.dma_start(dram("A1")(), given("A1")).then_inc(s.ldA, 16)
        g.scalar.dma_start(T.wp[:], T.ws[:]).then_inc(s.ok0, 16)
        g.sync.dma_start(T.wq[:].bitcast(u8), T.wc[:]).then_inc(s.ok0, 16)
        need[0] = 32
    if rank is not None:
        g.sync.dma_start(T.xt[:, 0:4 * NX], T.x[:, 0:4 * NX]).then_inc(s.x0, 16)
        g.scalar.dma_start(T.xt[:, 4 * NX:8 * NX], T.x[:, 4 * NX:8 * NX]).then_inc(s.x1, 16)

    if core == root:
        for p, ld in (("B", s.ldB), ("C", s.ldC)):
            g.wait_ge(ld, 16)
            call([(dram(p), dram(p), list(relays[p]), hand[p][0], hand[p][1], s.inT)])
        for k, (ld, rsem) in enumerate(((s.ldS, s.inS), (s.ldA, s.inA))):
            g.wait_ge(ld, 32)
            call([(dram((NEAR, FAR)[side][k]), dram((NEAR, FAR)[side][k]), dests, m, n, rsem)
                  for side, dests, m, n in off])
        if home:
            g.wait_ge(s.ok0, 32)
            call([(lambda: T.wp[:], lambda: T.wp[:], home, home_mask, home_n, s.ok0)])
            call([(lambda: T.wq[:].bitcast(u8), lambda: T.wq[:].bitcast(u8), home, home_mask, home_n, s.ok0)])
    for p in relays:
        if core in relays[p]:
            dests = relays[p][core]
            m, n = _engines(_common(topo, core, dests), SMALL)
            g.wait_ge(s.inT, hand[p][1])
            call([(dram(p), dram(p), _turn(dests, 2), m, n, s.inT)])
    if core in home:
        need[0] = 2 * home_n
    for pair in sites:
        if core in pair:
            side = pair.index(core)
            mate = pair[1 - side]
            mine = (NEAR, FAR)[side]
            m, n = _engines(topo.mask(core, mate), 16)
            last = [c for c in relays[mine[2]] if core in relays[mine[2]][c]][0]
            counts = (share, share, _engines(_common(topo, last, relays[mine[2]][last]), SMALL)[1])
            sems = (s.inS, s.inA, s.inT)
            for p, sem, cnt in zip(mine, sems, counts):
                g.wait_ge(sem, cnt)
                call([(dram(p), sbuf(p), [mate], m, n, ok(p))])
            for p, sem, cnt, q in zip(mine, sems, counts, (g.scalar, g.sync, g.scalar)):
                q.wait_ge(sem, cnt)
                q.dma_start(sbuf(p)(), dram(p)()).then_inc(ok(p), 16)
            n_back = _engines(topo.mask(mate, core), 16)[1]
            theirs = (NEAR, FAR)[1 - side]
            for k in (0, 1):
                need[k] = sum(16 for p in mine if (p in FIRST) == (k == 0)) \
                    + sum(n_back for p in theirs if (p in FIRST) == (k == 0))
    if sent[0]:
        g.wait_ge(s.sent, sent[0])
    if rank is None:
        return

    v, te = g.vector, g.tensor
    v.wait_ge(s.x0, 16)
    v.quantize_mx(T.xq[:, 0:NX], T.xs[:, 0:NX], T.xt[:, 0:4 * NX]).then_inc(s.q0, 1)
    v.wait_ge(s.x1, 16)
    v.quantize_mx(T.xq[:, NX:2 * NX], T.xs[:, NX:2 * NX], T.xt[:, 4 * NX:8 * NX]).then_inc(s.q1, 1)

    te.wait_ge(s.q0, 1)
    te.wait_ge(s.q1, 1)
    te.wait_ge(s.ok0, need[0])
    te.matmul_mx(T.ps[:, 0:NX], T.wq[:, 0:128], T.wp[:, 0:128], T.xq[:, 0:NX], T.xs[:, 0:NX], True, False)
    if need[1]:
        te.wait_ge(s.ok1, need[1])
    te.matmul_mx(T.ps[:, 0:NX], T.wq[:, 128:256], T.wp[:, 128:256], T.xq[:, NX:2 * NX], T.xs[:, NX:2 * NX],
                 False, True).then_inc(s.mm, 1)

    v.wait_ge(s.mm, 1)
    v.tensor_copy(T.yt[:], T.ps[:, 0:NX]).then_inc(s.cp, 1)
    g.sync.wait_ge(s.cp, 1)
    g.sync.dma_start(T.y[:], T.yt[:]).then_inc(s.st, 16)
    g.sync.wait_ge(s.st, 16)
